import numpy as np
import ml_dtypes


def mxq(x, axis, fmt="e4m3"):
    dtype, down = {"e4m3": (ml_dtypes.float8_e4m3fn, 7), "e5m2": (ml_dtypes.float8_e5m2, 14)}[fmt]
    v = np.moveaxis(np.asarray(x, np.float32).astype(ml_dtypes.bfloat16).astype(np.float64), axis, -1)
    blocks = v.reshape(v.shape[:-1] + (-1, 32))
    amax = np.abs(blocks).max(-1, keepdims=True)
    byte = np.maximum(np.where(amax > 0, np.frexp(amax)[1] - 1 + 127, 0) - down, 1)
    scale = np.exp2(byte - 127.0)
    codes = (blocks / scale).astype(np.float32).astype(dtype).astype(np.float64)
    return np.moveaxis((codes * scale).reshape(v.shape), -1, axis)


WIDE = False


def mx_kscale(k, group=512):
    if not WIDE:
        return np.ones(k)
    levels = np.array([18, -18])
    if group != 512:
        return np.exp2(np.random.permutation(np.resize(levels, k // group))).repeat(group)
    if k % 512:
        return np.exp2(np.random.permutation(np.resize(levels, k // 32))).repeat(32)
    a = np.empty((k // 512, 16))
    for p in range(k // 512):
        a[p, :8] = np.random.permutation(np.resize(levels, 8))
        for g in range(8):
            far = levels[np.abs(levels - a[p, g]) >= 10]
            a[p, g + 8] = far[np.random.randint(len(far))]
    return np.exp2(a.ravel()).repeat(32)


def f64(x):
    return np.asarray(x).astype(np.float64)


G, D, M, O, N = 4, 128, 128, 128, 512


def setup_inputs():
    n = np.random.standard_normal
    s_d = mx_kscale(D, 0)
    s_o = mx_kscale(O, 0)
    return {
        "x": (n((G, D, N)) * s_d[:, None]).astype(np.float32),
        "w1": (n((G, D, M)) / np.sqrt(D) / s_d[:, None]).astype(np.float32),
        "w2": (n((G, D, M)) / np.sqrt(D) / s_d[:, None]).astype(np.float32),
        "tp": (np.random.uniform(0.6, 2.0, (G, M, 1))).astype(np.float32),
        "wo": (n((G, O, M)) / np.sqrt(O) / s_o[:, None]).astype(np.float32),
        "dy": (n((G, O, N)) * s_o[:, None]).astype(np.float32),
        "old": (0.3 * n((G, M, N))).astype(np.float32),
    }


def reference(x, w1, w2, tp, wo, dy, old):
    w1q = mxq(f64(w1), 1, "e4m3")
    xq = mxq(f64(x), 1, "e4m3")
    z1 = w1q.transpose(0, 2, 1) @ xq
    w2q = mxq(f64(w2), 1, "e4m3")
    z2 = w2q.transpose(0, 2, 1) @ xq
    se = np.exp(z1 * f64(tp)) + np.exp(z2 * f64(tp))
    woq = mxq(f64(wo), 1, "e4m3")
    dyq = mxq(f64(dy), 1, "e4m3")
    c0 = woq.transpose(0, 2, 1) @ dyq
    dse = c0 / f64(tp) / se
    dz1 = dse * np.exp(z1 * f64(tp)) * f64(tp)
    y = dz1 + f64(old)
    return y

@@ -1,0 +1,169 @@
+from contextlib import ExitStack
+
+import concourse.mybir as mybir
+
+G, D, M, N = 4, 128, 128, 512
+FLOPS = 3 * 2 * G * D * M * N
+
+F32 = mybir.dt.float32
+BF16 = mybir.dt.bfloat16
+U32 = mybir.dt.uint32
+U8 = mybir.dt.uint8
+FP8X4 = mybir.dt.float8_e4m3fn_x4
+ACT = mybir.ActivationFunctionType
+ALU = mybir.AluOpType
+
+P = 128
+PACK = 4
+ROWS = D // PACK
+HALF = N // 2
+NT = 128
+RUN = 4
+SPLIT_XB = 96
+SPLIT_DYB = 152
+
+
+def tile_rows_bsoftmaxoftwo_kernel(tc, x, w1, w2, tp, wo, dy, old, out):
+    nc = tc.nc
+    with ExitStack() as ctx:
+        sb = ctx.enter_context(tc.tile_pool(name="sb", bufs=1))
+        ps = ctx.enter_context(tc.psum_pool(name="ps", bufs=1))
+        ctx.enter_context(tc.manual_schedule())
+
+        def operand(name, width):
+            return {
+                "raw": sb.tile([P, PACK, width], F32, name=name + "_raw", align_bytes=64),
+                "bf": sb.tile([P, width * PACK], BF16, name=name + "_bf", align_bytes=64),
+                "codes": sb.tile([P, width], U32, name=name + "_codes", align_bytes=64),
+                "scales": sb.tile([P, width], U8, name=name + "_scales", align_bytes=64),
+                "width": width,
+            }
+
+        def load(op, src, c0):
+            rows = src.rearrange("g (p j) n -> (g p) j n", j=PACK)
+            nc.sync.dma_start(out=op["raw"][:], in_=rows[:, :, c0 : c0 + op["width"]])
+
+        def views(op, c0, c1):
+            dst = op["bf"][:, PACK * c0 : PACK * c1].rearrange("p (c i j) -> p c j i", i=RUN, j=PACK)
+            src = op["raw"][:, :, c0:c1].rearrange("p j (c i) -> p c j i", i=RUN)
+            return dst, src
+
+        def round_vector(op, c0, c1):
+            dst, src = views(op, c0, c1)
+            nc.vector.tensor_copy(out=dst, in_=src)
+
+        def round_scalar(op, c0, c1):
+            dst, src = views(op, c0, c1)
+            nc.scalar.copy(out=dst, in_=src)
+
+        def quantize(op):
+            nc.vector.quantize_mx(out=op["codes"][:].bitcast(FP8X4), scales=op["scales"][:], in_=op["bf"][:])
+
+        def mx(dst, w, a, g, c0, start, stop):
+            r = slice(ROWS * g, ROWS * (g + 1))
+            nc.tensor.matmul_mx(
+                out=dst,
+                lhsT=w["codes"][r, :].bitcast(FP8X4),
+                lhsT_scale=w["scales"][r, :],
+                rhs=a["codes"][r, c0 : c0 + NT].bitcast(FP8X4),
+                rhs_scale=a["scales"][r, c0 : c0 + NT],
+                start=start,
+                stop=stop,
+            )
+
+        xs = [operand("x%d" % h, HALF) for h in range(2)]
+        dys = [operand("dy%d" % h, HALF) for h in range(2)]
+        w1o = operand("w1", M)
+        w2o = operand("w2", M)
+        woo = operand("wo", M)
+        olds = [sb.tile([P, N], F32, name="old%d" % g, align_bytes=64) for g in range(G)]
+        gate = [[sb.tile([P, HALF], F32, name="gate%d_%d" % (g, h), align_bytes=64) for h in range(2)] for g in range(G)]
+        prod = [sb.tile([P, N], F32, name="prod%d" % g, align_bytes=64) for g in range(G)]
+        res = [sb.tile([P, N], F32, name="res%d" % g, align_bytes=64) for g in range(G)]
+        zb = [ps.tile([P, N], F32, name="z%d" % g) for g in range(G)]
+        cb = [ps.tile([P, N], F32, name="c%d" % g) for g in range(G)]
+        tp_rows = sb.tile([P, P], F32, align_bytes=64)
+        tp_cols = sb.tile([P, P], F32, align_bytes=64)
+        warm_in = sb.tile([P, 8], F32, align_bytes=64)
+        warm_out = sb.tile([P, 8], F32, align_bytes=64)
+
+        def diff_products(h):
+            for b in range(HALF // NT):
+                for first in (True, False):
+                    for g in range(G):
+                        c = h * HALF + b * NT
+                        mx(zb[g][:, c : c + NT], w1o if first else w2o, xs[h], g, b * NT, first, not first)
+
+        def grad_products(h):
+            for b in range(HALF // NT):
+                for g in range(G):
+                    c = h * HALF + b * NT
+                    mx(cb[g][:, c : c + NT], woo, dys[h], g, b * NT, True, True)
+
+        def sigmoid(g, h):
+            nc.scalar.activation(
+                out=gate[g][h][:], in_=zb[g][:, h * HALF : (h + 1) * HALF], func=ACT.Sigmoid,
+                scale=tp_cols[:, ROWS * g : ROWS * g + 1],
+            )
+
+        def multiply(g, h):
+            cols = slice(h * HALF, (h + 1) * HALF)
+            nc.vector.tensor_tensor(out=prod[g][:, cols], in0=cb[g][:, cols], in1=gate[g][h][:], op=ALU.mult)
+
+        def add_and_store(g):
+            nc.vector.tensor_tensor(out=res[g][:], in0=prod[g][:], in1=olds[g][:], op=ALU.add)
+            nc.sync.dma_start(out=out[g], in_=res[g][:])
+
+        nc.vector.memset(tp_rows[:], 0.0)
+        nc.vector.memset(warm_in[:], 0.0)
+        load(xs[0], x, 0)
+        nc.scalar.dma_start(
+            out=tp_rows[0:P:32, :].rearrange("q (g i) -> q g i", g=G),
+            in_=tp.rearrange("g (q i) o -> q g (i o)", i=32),
+        )
+        load(w1o, w1, 0)
+        load(w2o, w2, 0)
+        load(woo, wo, 0)
+        load(dys[0], dy, 0)
+        load(xs[1], x, HALF)
+        load(dys[1], dy, HALF)
+        for g in range(G):
+            nc.sync.dma_start(out=olds[g][:], in_=old[g])
+
+        nc.scalar.activation(out=warm_out[:], in_=warm_in[:], func=ACT.Sigmoid)
+        nc.vector.transpose(out=tp_cols[:], in_=tp_rows[:])
+
+        round_vector(xs[0], 0, HALF)
+        round_scalar(w1o, 0, M)
+        quantize(xs[0])
+        dst, src = views(w2o, 0, M)
+        nc.vector.tensor_scalar(out=dst, in0=src, scalar1=-1.0, scalar2=None, op0=ALU.mult)
+        quantize(w1o)
+        quantize(w2o)
+        diff_products(0)
+        round_vector(woo, 0, M)
+        quantize(woo)
+        for g in range(G):
+            sigmoid(g, 0)
+        round_vector(dys[0], 0, HALF)
+        quantize(dys[0])
+        grad_products(0)
+        round_vector(xs[1], 0, SPLIT_XB)
+        round_scalar(xs[1], SPLIT_XB, HALF)
+        multiply(0, 0)
+        quantize(xs[1])
+        diff_products(1)
+        multiply(1, 0)
+        round_vector(dys[1], 0, SPLIT_DYB)
+        round_scalar(dys[1], SPLIT_DYB, HALF)
+        multiply(2, 0)
+        quantize(dys[1])
+        multiply(3, 0)
+        grad_products(1)
+        for g in range(G):
+            sigmoid(g, 1)
+        multiply(0, 1)
+        for g in range(G):
+            if g + 1 < G:
+                multiply(g + 1, 1)
+            add_and_store(g)

@@ -17,10 +17,10 @@ P = 128
 PACK = 4
 ROWS = D // PACK
 HALF = N // 2
-NT = 128
 RUN = 4
-SPLIT_XB = 96
-SPLIT_DYB = 152
+SPLIT_X = 328
+SPLIT_DYA = 160
+SPLIT_DYB = 160
 
 
 def tile_rows_bsoftmaxoftwo_kernel(tc, x, w1, w2, tp, wo, dy, old, out):
@@ -30,12 +30,17 @@ def tile_rows_bsoftmaxoftwo_kernel(tc, x, w1, w2, tp, wo, dy, old, out):
         ps = ctx.enter_context(tc.psum_pool(name="ps", bufs=1))
         ctx.enter_context(tc.manual_schedule())
 
-        def operand(name, width):
+        def planes(name, width):
+            codes = sb.tile([P, width], U32, name=name + "_codes", align_bytes=64)
+            scales = sb.tile([P, width], U8, name=name + "_scales", align_bytes=64)
+            return codes, scales
+
+        def operand(name, width, pl, c0):
             return {
                 "raw": sb.tile([P, PACK, width], F32, name=name + "_raw", align_bytes=64),
                 "bf": sb.tile([P, width * PACK], BF16, name=name + "_bf", align_bytes=64),
-                "codes": sb.tile([P, width], U32, name=name + "_codes", align_bytes=64),
-                "scales": sb.tile([P, width], U8, name=name + "_scales", align_bytes=64),
+                "codes": pl[0][:, c0 : c0 + width],
+                "scales": pl[1][:, c0 : c0 + width],
                 "width": width,
             }
 
@@ -57,27 +62,29 @@ def tile_rows_bsoftmaxoftwo_kernel(tc, x, w1, w2, tp, wo, dy, old, out):
             nc.scalar.copy(out=dst, in_=src)
 
         def quantize(op):
-            nc.vector.quantize_mx(out=op["codes"][:].bitcast(FP8X4), scales=op["scales"][:], in_=op["bf"][:])
+            nc.vector.quantize_mx(out=op["codes"].bitcast(FP8X4), scales=op["scales"], in_=op["bf"][:])
 
-        def mx(dst, w, a, g, c0, start, stop):
+        def mx(dst, w, a, g, start, stop):
             r = slice(ROWS * g, ROWS * (g + 1))
             nc.tensor.matmul_mx(
                 out=dst,
-                lhsT=w["codes"][r, :].bitcast(FP8X4),
-                lhsT_scale=w["scales"][r, :],
-                rhs=a["codes"][r, c0 : c0 + NT].bitcast(FP8X4),
-                rhs_scale=a["scales"][r, c0 : c0 + NT],
+                lhsT=w[0][r, :].bitcast(FP8X4),
+                lhsT_scale=w[1][r, :],
+                rhs=a[0][r, :].bitcast(FP8X4),
+                rhs_scale=a[1][r, :],
                 start=start,
                 stop=stop,
             )
 
-        xs = [operand("x%d" % h, HALF) for h in range(2)]
-        dys = [operand("dy%d" % h, HALF) for h in range(2)]
-        w1o = operand("w1", M)
-        w2o = operand("w2", M)
-        woo = operand("wo", M)
+        xp, dyp = planes("x", N), planes("dy", N)
+        w1p, w2p, wop = planes("w1", M), planes("w2", M), planes("wo", M)
+        xo = operand("x", N, xp, 0)
+        dys = [operand("dy%d" % h, HALF, dyp, h * HALF) for h in range(2)]
+        w1o = operand("w1", M, w1p, 0)
+        w2o = operand("w2", M, w2p, 0)
+        woo = operand("wo", M, wop, 0)
         olds = [sb.tile([P, N], F32, name="old%d" % g, align_bytes=64) for g in range(G)]
-        gate = [[sb.tile([P, HALF], F32, name="gate%d_%d" % (g, h), align_bytes=64) for h in range(2)] for g in range(G)]
+        gate = [sb.tile([P, N], F32, name="gate%d" % g, align_bytes=64) for g in range(G)]
         prod = [sb.tile([P, N], F32, name="prod%d" % g, align_bytes=64) for g in range(G)]
         res = [sb.tile([P, N], F32, name="res%d" % g, align_bytes=64) for g in range(G)]
         zb = [ps.tile([P, N], F32, name="z%d" % g) for g in range(G)]
@@ -87,83 +94,64 @@ def tile_rows_bsoftmaxoftwo_kernel(tc, x, w1, w2, tp, wo, dy, old, out):
         warm_in = sb.tile([P, 8], F32, align_bytes=64)
         warm_out = sb.tile([P, 8], F32, align_bytes=64)
 
-        def diff_products(h):
-            for b in range(HALF // NT):
-                for first in (True, False):
-                    for g in range(G):
-                        c = h * HALF + b * NT
-                        mx(zb[g][:, c : c + NT], w1o if first else w2o, xs[h], g, b * NT, first, not first)
+        def sigmoid(g):
+            nc.scalar.activation(out=gate[g][:], in_=zb[g][:], func=ACT.Sigmoid, scale=tp_cols[:, ROWS * g : ROWS * g + 1])
 
-        def grad_products(h):
-            for b in range(HALF // NT):
-                for g in range(G):
-                    c = h * HALF + b * NT
-                    mx(cb[g][:, c : c + NT], woo, dys[h], g, b * NT, True, True)
+        def multiply(g):
+            nc.vector.tensor_tensor(out=prod[g][:], in0=cb[g][:], in1=gate[g][:], op=ALU.mult)
 
-        def sigmoid(g, h):
-            nc.scalar.activation(
-                out=gate[g][h][:], in_=zb[g][:, h * HALF : (h + 1) * HALF], func=ACT.Sigmoid,
-                scale=tp_cols[:, ROWS * g : ROWS * g + 1],
-            )
+        def add(eng, g, c0, c1):
+            eng.tensor_tensor(out=res[g][:, c0:c1], in0=prod[g][:, c0:c1], in1=olds[g][:, c0:c1], op=ALU.add)
 
-        def multiply(g, h):
-            cols = slice(h * HALF, (h + 1) * HALF)
-            nc.vector.tensor_tensor(out=prod[g][:, cols], in0=cb[g][:, cols], in1=gate[g][h][:], op=ALU.mult)
+        def store(g, c0, c1):
+            nc.sync.dma_start(out=out[g][:, c0:c1], in_=res[g][:, c0:c1])
 
-        def add_and_store(g):
-            nc.vector.tensor_tensor(out=res[g][:], in0=prod[g][:], in1=olds[g][:], op=ALU.add)
-            nc.sync.dma_start(out=out[g], in_=res[g][:])
-
-        nc.vector.memset(tp_rows[:], 0.0)
+        nc.gpsimd.memset(tp_rows[:], 0.0)
         nc.vector.memset(warm_in[:], 0.0)
-        load(xs[0], x, 0)
+        load(w1o, w1, 0)
         nc.scalar.dma_start(
             out=tp_rows[0:P:32, :].rearrange("q (g i) -> q g i", g=G),
             in_=tp.rearrange("g (q i) o -> q g (i o)", i=32),
         )
-        load(w1o, w1, 0)
         load(w2o, w2, 0)
+        load(xo, x, 0)
         load(woo, wo, 0)
         load(dys[0], dy, 0)
-        load(xs[1], x, HALF)
         load(dys[1], dy, HALF)
         for g in range(G):
             nc.sync.dma_start(out=olds[g][:], in_=old[g])
 
         nc.scalar.activation(out=warm_out[:], in_=warm_in[:], func=ACT.Sigmoid)
-        nc.vector.transpose(out=tp_cols[:], in_=tp_rows[:])
 
-        round_vector(xs[0], 0, HALF)
-        round_scalar(w1o, 0, M)
-        quantize(xs[0])
+        round_vector(w1o, 0, M)
         dst, src = views(w2o, 0, M)
         nc.vector.tensor_scalar(out=dst, in0=src, scalar1=-1.0, scalar2=None, op0=ALU.mult)
         quantize(w1o)
+        nc.vector.transpose(out=tp_cols[:], in_=tp_rows[:])
         quantize(w2o)
-        diff_products(0)
-        round_vector(woo, 0, M)
-        quantize(woo)
+        round_vector(xo, 0, SPLIT_X)
+        round_scalar(xo, SPLIT_X, N)
+        round_scalar(woo, 0, M)
+        quantize(xo)
         for g in range(G):
-            sigmoid(g, 0)
-        round_vector(dys[0], 0, HALF)
+            mx(zb[g][:], w1p, xp, g, True, False)
+            mx(zb[g][:], w2p, xp, g, False, True)
+        quantize(woo)
+        round_vector(dys[0], 0, SPLIT_DYA)
+        round_scalar(dys[0], SPLIT_DYA, HALF)
         quantize(dys[0])
-        grad_products(0)
-        round_vector(xs[1], 0, SPLIT_XB)
-        round_scalar(xs[1], SPLIT_XB, HALF)
-        multiply(0, 0)
-        quantize(xs[1])
-        diff_products(1)
-        multiply(1, 0)
         round_vector(dys[1], 0, SPLIT_DYB)
         round_scalar(dys[1], SPLIT_DYB, HALF)
-        multiply(2, 0)
         quantize(dys[1])
-        multiply(3, 0)
-        grad_products(1)
         for g in range(G):
-            sigmoid(g, 1)
-        multiply(0, 1)
+            mx(cb[g][:], wop, dyp, g, True, True)
         for g in range(G):
-            if g + 1 < G:
-                multiply(g + 1, 1)
-            add_and_store(g)
+            sigmoid(g)
+        multiply(0)
+        for g in range(G - 1):
+            multiply(g + 1)
+            add(nc.vector, g, 0, N)
+            store(g, 0, N)
+        for c0 in (0, HALF):
+            add(nc.vector, G - 1, c0, c0 + HALF)
+            store(G - 1, c0, c0 + HALF)

@@ -18,9 +18,9 @@ PACK = 4
 ROWS = D // PACK
 HALF = N // 2
 RUN = 4
-SPLIT_X = 328
-SPLIT_DYA = 160
-SPLIT_DYB = 160
+SCALAR_X = 184
+SCALAR_DY = 176
+POOL_COLS = 160
 
 
 def tile_rows_bsoftmaxoftwo_kernel(tc, x, w1, w2, tp, wo, dy, old, out):
@@ -30,23 +30,16 @@ def tile_rows_bsoftmaxoftwo_kernel(tc, x, w1, w2, tp, wo, dy, old, out):
         ps = ctx.enter_context(tc.psum_pool(name="ps", bufs=1))
         ctx.enter_context(tc.manual_schedule())
 
-        def planes(name, width):
-            codes = sb.tile([P, width], U32, name=name + "_codes", align_bytes=64)
-            scales = sb.tile([P, width], U8, name=name + "_scales", align_bytes=64)
-            return codes, scales
-
-        def operand(name, width, pl, c0):
+        def operand(name, width):
             return {
                 "raw": sb.tile([P, PACK, width], F32, name=name + "_raw", align_bytes=64),
                 "bf": sb.tile([P, width * PACK], BF16, name=name + "_bf", align_bytes=64),
-                "codes": pl[0][:, c0 : c0 + width],
-                "scales": pl[1][:, c0 : c0 + width],
-                "width": width,
+                "codes": sb.tile([P, width], U32, name=name + "_codes", align_bytes=64),
+                "scales": sb.tile([P, width], U8, name=name + "_scales", align_bytes=64),
             }
 
-        def load(op, src, c0):
-            rows = src.rearrange("g (p j) n -> (g p) j n", j=PACK)
-            nc.sync.dma_start(out=op["raw"][:], in_=rows[:, :, c0 : c0 + op["width"]])
+        def load(op, src):
+            nc.sync.dma_start(out=op["raw"][:], in_=src.rearrange("g (p j) n -> (g p) j n", j=PACK))
 
         def views(op, c0, c1):
             dst = op["bf"][:, PACK * c0 : PACK * c1].rearrange("p (c i j) -> p c j i", i=RUN, j=PACK)
@@ -61,28 +54,34 @@ def tile_rows_bsoftmaxoftwo_kernel(tc, x, w1, w2, tp, wo, dy, old, out):
             dst, src = views(op, c0, c1)
             nc.scalar.copy(out=dst, in_=src)
 
-        def quantize(op):
-            nc.vector.quantize_mx(out=op["codes"].bitcast(FP8X4), scales=op["scales"], in_=op["bf"][:])
+        def quantize(op, c0, c1):
+            nc.vector.quantize_mx(
+                out=op["codes"][:, c0:c1].bitcast(FP8X4),
+                scales=op["scales"][:, c0:c1],
+                in_=op["bf"][:, PACK * c0 : PACK * c1],
+            )
+
+        def round_and_quantize(op, scalar_cols):
+            round_vector(op, 0, HALF)
+            round_scalar(op, HALF, HALF + scalar_cols)
+            round_vector(op, HALF + scalar_cols, N)
+            quantize(op, 0, HALF)
+            quantize(op, HALF, N)
 
         def mx(dst, w, a, g, start, stop):
             r = slice(ROWS * g, ROWS * (g + 1))
             nc.tensor.matmul_mx(
                 out=dst,
-                lhsT=w[0][r, :].bitcast(FP8X4),
-                lhsT_scale=w[1][r, :],
-                rhs=a[0][r, :].bitcast(FP8X4),
-                rhs_scale=a[1][r, :],
+                lhsT=w["codes"][r, :].bitcast(FP8X4),
+                lhsT_scale=w["scales"][r, :],
+                rhs=a["codes"][r, :].bitcast(FP8X4),
+                rhs_scale=a["scales"][r, :],
                 start=start,
                 stop=stop,
             )
 
-        xp, dyp = planes("x", N), planes("dy", N)
-        w1p, w2p, wop = planes("w1", M), planes("w2", M), planes("wo", M)
-        xo = operand("x", N, xp, 0)
-        dys = [operand("dy%d" % h, HALF, dyp, h * HALF) for h in range(2)]
-        w1o = operand("w1", M, w1p, 0)
-        w2o = operand("w2", M, w2p, 0)
-        woo = operand("wo", M, wop, 0)
+        xo, dyo = operand("x", N), operand("dy", N)
+        w1o, w2o, woo = operand("w1", M), operand("w2", M), operand("wo", M)
         olds = [sb.tile([P, N], F32, name="old%d" % g, align_bytes=64) for g in range(G)]
         gate = [sb.tile([P, N], F32, name="gate%d" % g, align_bytes=64) for g in range(G)]
         prod = [sb.tile([P, N], F32, name="prod%d" % g, align_bytes=64) for g in range(G)]
@@ -94,11 +93,18 @@ def tile_rows_bsoftmaxoftwo_kernel(tc, x, w1, w2, tp, wo, dy, old, out):
         warm_in = sb.tile([P, 8], F32, align_bytes=64)
         warm_out = sb.tile([P, 8], F32, align_bytes=64)
 
-        def sigmoid(g):
-            nc.scalar.activation(out=gate[g][:], in_=zb[g][:], func=ACT.Sigmoid, scale=tp_cols[:, ROWS * g : ROWS * g + 1])
+        def difference(g):
+            mx(zb[g][:], w1o, xo, g, True, False)
+            mx(zb[g][:], w2o, xo, g, False, True)
 
-        def multiply(g):
-            nc.vector.tensor_tensor(out=prod[g][:], in0=cb[g][:], in1=gate[g][:], op=ALU.mult)
+        def gradient(g):
+            mx(cb[g][:], woo, dyo, g, True, True)
+
+        def sigmoid(g, c0, c1):
+            nc.scalar.activation(out=gate[g][:, c0:c1], in_=zb[g][:, c0:c1], func=ACT.Sigmoid, scale=tp_cols[:, ROWS * g : ROWS * g + 1])
+
+        def multiply(g, c0, c1):
+            nc.vector.tensor_tensor(out=prod[g][:, c0:c1], in0=cb[g][:, c0:c1], in1=gate[g][:, c0:c1], op=ALU.mult)
 
         def add(eng, g, c0, c1):
             eng.tensor_tensor(out=res[g][:, c0:c1], in0=prod[g][:, c0:c1], in1=olds[g][:, c0:c1], op=ALU.add)
@@ -108,50 +114,55 @@ def tile_rows_bsoftmaxoftwo_kernel(tc, x, w1, w2, tp, wo, dy, old, out):
 
         nc.gpsimd.memset(tp_rows[:], 0.0)
         nc.vector.memset(warm_in[:], 0.0)
-        load(w1o, w1, 0)
+        load(xo, x)
         nc.scalar.dma_start(
             out=tp_rows[0:P:32, :].rearrange("q (g i) -> q g i", g=G),
             in_=tp.rearrange("g (q i) o -> q g (i o)", i=32),
         )
-        load(w2o, w2, 0)
-        load(xo, x, 0)
-        load(woo, wo, 0)
-        load(dys[0], dy, 0)
-        load(dys[1], dy, HALF)
+        load(w1o, w1)
+        load(w2o, w2)
+        load(dyo, dy)
+        load(woo, wo)
         for g in range(G):
             nc.sync.dma_start(out=olds[g][:], in_=old[g])
 
         nc.scalar.activation(out=warm_out[:], in_=warm_in[:], func=ACT.Sigmoid)
 
-        round_vector(w1o, 0, M)
+        round_and_quantize(xo, SCALAR_X)
+        round_scalar(w1o, 0, M)
         dst, src = views(w2o, 0, M)
-        nc.vector.tensor_scalar(out=dst, in0=src, scalar1=-1.0, scalar2=None, op0=ALU.mult)
-        quantize(w1o)
+        nc.scalar.activation(out=dst, in_=src, func=ACT.Copy, scale=-1.0)
+        quantize(w1o, 0, M)
+        quantize(w2o, 0, M)
         nc.vector.transpose(out=tp_cols[:], in_=tp_rows[:])
-        quantize(w2o)
-        round_vector(xo, 0, SPLIT_X)
-        round_scalar(xo, SPLIT_X, N)
-        round_scalar(woo, 0, M)
-        quantize(xo)
-        for g in range(G):
-            mx(zb[g][:], w1p, xp, g, True, False)
-            mx(zb[g][:], w2p, xp, g, False, True)
-        quantize(woo)
-        round_vector(dys[0], 0, SPLIT_DYA)
-        round_scalar(dys[0], SPLIT_DYA, HALF)
-        quantize(dys[0])
-        round_vector(dys[1], 0, SPLIT_DYB)
-        round_scalar(dys[1], SPLIT_DYB, HALF)
-        quantize(dys[1])
-        for g in range(G):
-            mx(cb[g][:], wop, dyp, g, True, True)
-        for g in range(G):
-            sigmoid(g)
-        multiply(0)
         for g in range(G - 1):
-            multiply(g + 1)
-            add(nc.vector, g, 0, N)
-            store(g, 0, N)
+            difference(g)
+        round_and_quantize(dyo, SCALAR_DY)
+        round_scalar(woo, 0, M)
+        quantize(woo, 0, M)
+        for g in range(G - 1):
+            gradient(g)
+            sigmoid(g, 0, N)
+        difference(G - 1)
+        gradient(G - 1)
         for c0 in (0, HALF):
-            add(nc.vector, G - 1, c0, c0 + HALF)
-            store(G - 1, c0, c0 + HALF)
+            sigmoid(G - 1, c0, c0 + HALF)
+        cut = N - POOL_COLS
+        for c0 in (0, HALF):
+            multiply(0, c0, c0 + HALF)
+            add(nc.gpsimd, 0, c0, c0 + HALF)
+        store(0, 0, N)
+        multiply(1, 0, N)
+        multiply(2, 0, cut)
+        add(nc.vector, 1, 0, N)
+        store(1, 0, N)
+        add(nc.vector, 2, 0, cut)
+        store(2, 0, cut)
+        multiply(2, cut, N)
+        add(nc.gpsimd, 2, cut, N)
+        store(2, cut, N)
+        for c0 in (0, HALF):
+            multiply(3, c0, c0 + HALF)
+        for c0 in (0, HALF):
+            add(nc.vector, 3, c0, c0 + HALF)
+            store(3, c0, c0 + HALF)

@@ -20,7 +20,6 @@ HALF = N // 2
 RUN = 4
 SCALAR_X = 184
 SCALAR_DY = 176
-POOL_COLS = 160
 
 
 def tile_rows_bsoftmaxoftwo_kernel(tc, x, w1, w2, tp, wo, dy, old, out):
@@ -106,10 +105,8 @@ def tile_rows_bsoftmaxoftwo_kernel(tc, x, w1, w2, tp, wo, dy, old, out):
         def multiply(g, c0, c1):
             nc.vector.tensor_tensor(out=prod[g][:, c0:c1], in0=cb[g][:, c0:c1], in1=gate[g][:, c0:c1], op=ALU.mult)
 
-        def add(eng, g, c0, c1):
-            eng.tensor_tensor(out=res[g][:, c0:c1], in0=prod[g][:, c0:c1], in1=olds[g][:, c0:c1], op=ALU.add)
-
-        def store(g, c0, c1):
+        def add_and_store(g, c0, c1):
+            nc.vector.tensor_tensor(out=res[g][:, c0:c1], in0=prod[g][:, c0:c1], in1=olds[g][:, c0:c1], op=ALU.add)
             nc.sync.dma_start(out=out[g][:, c0:c1], in_=res[g][:, c0:c1])
 
         nc.gpsimd.memset(tp_rows[:], 0.0)
@@ -147,22 +144,13 @@ def tile_rows_bsoftmaxoftwo_kernel(tc, x, w1, w2, tp, wo, dy, old, out):
         gradient(G - 1)
         for c0 in (0, HALF):
             sigmoid(G - 1, c0, c0 + HALF)
-        cut = N - POOL_COLS
-        for c0 in (0, HALF):
-            multiply(0, c0, c0 + HALF)
-            add(nc.gpsimd, 0, c0, c0 + HALF)
-        store(0, 0, N)
-        multiply(1, 0, N)
-        multiply(2, 0, cut)
-        add(nc.vector, 1, 0, N)
-        store(1, 0, N)
-        add(nc.vector, 2, 0, cut)
-        store(2, 0, cut)
-        multiply(2, cut, N)
-        add(nc.gpsimd, 2, cut, N)
-        store(2, cut, N)
-        for c0 in (0, HALF):
-            multiply(3, c0, c0 + HALF)
-        for c0 in (0, HALF):
-            add(nc.vector, 3, c0, c0 + HALF)
-            store(3, c0, c0 + HALF)
+        last = G - 1
+        multiply(0, 0, N)
+        for g in range(1, last):
+            multiply(g, 0, N)
+            add_and_store(g - 1, 0, N)
+        multiply(last, 0, HALF)
+        add_and_store(last - 1, 0, N)
+        multiply(last, HALF, N)
+        add_and_store(last, 0, HALF)
+        add_and_store(last, HALF, N)

from contextlib import ExitStack

import concourse.mybir as mybir

G, D, M, N = 4, 128, 128, 512
FLOPS = 3 * 2 * G * D * M * N

F32 = mybir.dt.float32
BF16 = mybir.dt.bfloat16
U32 = mybir.dt.uint32
U8 = mybir.dt.uint8
FP8X4 = mybir.dt.float8_e4m3fn_x4
ACT = mybir.ActivationFunctionType
ALU = mybir.AluOpType

P = 128
PACK = 4
ROWS = D // PACK
HALF = N // 2
RUN = 4
SCALAR_X = 184
SCALAR_DY = 176


def tile_rows_bsoftmaxoftwo_kernel(tc, x, w1, w2, tp, wo, dy, old, out):
    nc = tc.nc
    with ExitStack() as ctx:
        sb = ctx.enter_context(tc.tile_pool(name="sb", bufs=1))
        ps = ctx.enter_context(tc.psum_pool(name="ps", bufs=1))
        ctx.enter_context(tc.manual_schedule())

        def operand(name, width):
            return {
                "raw": sb.tile([P, PACK, width], F32, name=name + "_raw", align_bytes=64),
                "bf": sb.tile([P, width * PACK], BF16, name=name + "_bf", align_bytes=64),
                "codes": sb.tile([P, width], U32, name=name + "_codes", align_bytes=64),
                "scales": sb.tile([P, width], U8, name=name + "_scales", align_bytes=64),
            }

        def load(op, src):
            nc.sync.dma_start(out=op["raw"][:], in_=src.rearrange("g (p j) n -> (g p) j n", j=PACK))

        def views(op, c0, c1):
            dst = op["bf"][:, PACK * c0 : PACK * c1].rearrange("p (c i j) -> p c j i", i=RUN, j=PACK)
            src = op["raw"][:, :, c0:c1].rearrange("p j (c i) -> p c j i", i=RUN)
            return dst, src

        def round_vector(op, c0, c1):
            dst, src = views(op, c0, c1)
            nc.vector.tensor_copy(out=dst, in_=src)

        def round_scalar(op, c0, c1):
            dst, src = views(op, c0, c1)
            nc.scalar.copy(out=dst, in_=src)

        def quantize(op, c0, c1):
            nc.vector.quantize_mx(
                out=op["codes"][:, c0:c1].bitcast(FP8X4),
                scales=op["scales"][:, c0:c1],
                in_=op["bf"][:, PACK * c0 : PACK * c1],
            )

        def round_and_quantize(op, scalar_cols):
            round_vector(op, 0, HALF)
            round_scalar(op, HALF, HALF + scalar_cols)
            round_vector(op, HALF + scalar_cols, N)
            quantize(op, 0, HALF)
            quantize(op, HALF, N)

        def mx(dst, w, a, g, start, stop):
            r = slice(ROWS * g, ROWS * (g + 1))
            nc.tensor.matmul_mx(
                out=dst,
                lhsT=w["codes"][r, :].bitcast(FP8X4),
                lhsT_scale=w["scales"][r, :],
                rhs=a["codes"][r, :].bitcast(FP8X4),
                rhs_scale=a["scales"][r, :],
                start=start,
                stop=stop,
            )

        xo, dyo = operand("x", N), operand("dy", N)
        w1o, w2o, woo = operand("w1", M), operand("w2", M), operand("wo", M)
        olds = [sb.tile([P, N], F32, name="old%d" % g, align_bytes=64) for g in range(G)]
        gate = [sb.tile([P, N], F32, name="gate%d" % g, align_bytes=64) for g in range(G)]
        prod = [sb.tile([P, N], F32, name="prod%d" % g, align_bytes=64) for g in range(G)]
        res = [sb.tile([P, N], F32, name="res%d" % g, align_bytes=64) for g in range(G)]
        zb = [ps.tile([P, N], F32, name="z%d" % g) for g in range(G)]
        cb = [ps.tile([P, N], F32, name="c%d" % g) for g in range(G)]
        tp_rows = sb.tile([P, P], F32, align_bytes=64)
        tp_cols = sb.tile([P, P], F32, align_bytes=64)
        warm_in = sb.tile([P, 8], F32, align_bytes=64)
        warm_out = sb.tile([P, 8], F32, align_bytes=64)

        def difference(g):
            mx(zb[g][:], w1o, xo, g, True, False)
            mx(zb[g][:], w2o, xo, g, False, True)

        def gradient(g):
            mx(cb[g][:], woo, dyo, g, True, True)

        def sigmoid(g, c0, c1):
            nc.scalar.activation(out=gate[g][:, c0:c1], in_=zb[g][:, c0:c1], func=ACT.Sigmoid, scale=tp_cols[:, ROWS * g : ROWS * g + 1])

        def multiply(g, c0, c1):
            nc.vector.tensor_tensor(out=prod[g][:, c0:c1], in0=cb[g][:, c0:c1], in1=gate[g][:, c0:c1], op=ALU.mult)

        def add_and_store(g, c0, c1):
            nc.vector.tensor_tensor(out=res[g][:, c0:c1], in0=prod[g][:, c0:c1], in1=olds[g][:, c0:c1], op=ALU.add)
            nc.sync.dma_start(out=out[g][:, c0:c1], in_=res[g][:, c0:c1])

        nc.gpsimd.memset(tp_rows[:], 0.0)
        nc.vector.memset(warm_in[:], 0.0)
        load(xo, x)
        nc.scalar.dma_start(
            out=tp_rows[0:P:32, :].rearrange("q (g i) -> q g i", g=G),
            in_=tp.rearrange("g (q i) o -> q g (i o)", i=32),
        )
        load(w1o, w1)
        load(w2o, w2)
        load(dyo, dy)
        load(woo, wo)
        for g in range(G):
            nc.sync.dma_start(out=olds[g][:], in_=old[g])

        nc.scalar.activation(out=warm_out[:], in_=warm_in[:], func=ACT.Sigmoid)

        round_and_quantize(xo, SCALAR_X)
        round_scalar(w1o, 0, M)
        dst, src = views(w2o, 0, M)
        nc.scalar.activation(out=dst, in_=src, func=ACT.Copy, scale=-1.0)
        quantize(w1o, 0, M)
        quantize(w2o, 0, M)
        nc.vector.transpose(out=tp_cols[:], in_=tp_rows[:])
        for g in range(G - 1):
            difference(g)
        round_and_quantize(dyo, SCALAR_DY)
        round_scalar(woo, 0, M)
        quantize(woo, 0, M)
        for g in range(G - 1):
            gradient(g)
            sigmoid(g, 0, N)
        difference(G - 1)
        gradient(G - 1)
        for c0 in (0, HALF):
            sigmoid(G - 1, c0, c0 + HALF)
        last = G - 1
        multiply(0, 0, N)
        for g in range(1, last):
            multiply(g, 0, N)
            add_and_store(g - 1, 0, N)
        multiply(last, 0, HALF)
        add_and_store(last - 1, 0, N)
        multiply(last, HALF, N)
        add_and_store(last, 0, HALF)
        add_and_store(last, HALF, N)
